import numpy as np
import ml_dtypes


def mxq(x, axis, fmt="e4m3"):
    dtype, down = {"e4m3": (ml_dtypes.float8_e4m3fn, 7), "e5m2": (ml_dtypes.float8_e5m2, 14)}[fmt]
    v = np.moveaxis(np.asarray(x, np.float32).astype(ml_dtypes.bfloat16).astype(np.float64), axis, -1)
    blocks = v.reshape(v.shape[:-1] + (-1, 32))
    amax = np.abs(blocks).max(-1, keepdims=True)
    byte = np.maximum(np.where(amax > 0, np.frexp(amax)[1] - 1 + 127, 0) - down, 1)
    scale = np.exp2(byte - 127.0)
    codes = (blocks / scale).astype(np.float32).astype(dtype).astype(np.float64)
    return np.moveaxis((codes * scale).reshape(v.shape), -1, axis)


WIDE = False


def mx_kscale(k):
    if not WIDE:
        return np.ones(k)
    levels = np.array([10, -10, 5, -5, 0])
    if k % 512:
        return np.exp2(np.random.permutation(np.resize(levels, k // 32))).repeat(32)
    a = np.empty((k // 512, 16))
    for p in range(k // 512):
        a[p, :8] = np.random.permutation(np.resize(levels, 8))
        for g in range(8):
            far = levels[np.abs(levels - a[p, g]) >= 10]
            a[p, g + 8] = far[np.random.randint(len(far))]
    return np.exp2(a.ravel()).repeat(32)


def f64(x):
    return np.asarray(x).astype(np.float64)


def striped(idx):
    return np.tile(idx.reshape(-1, 16).T, (8, 1)).astype(np.uint16)


def unstriped(offs):
    return offs[:16].T.reshape(-1).astype(np.int64)


def pack_weight(w):
    k, n = w.shape
    w = f64(np.asarray(w, np.float32).astype(ml_dtypes.bfloat16)).reshape(k // 32, 32, n)
    amax = np.abs(w).max(1)
    byte = np.clip(np.where(amax > 0, np.frexp(amax)[1] - 1 + 127 - 7, 1), 1, 254)
    scaled = (w * np.exp2(127.0 - byte)[:, None, :]).reshape(k, n).astype(np.float32)
    words = np.ascontiguousarray(scaled.reshape(k // 512, 128, 4, n).transpose(0, 1, 3, 2)).astype(ml_dtypes.float8_e4m3fn).view(np.uint8)
    return words, np.ascontiguousarray(byte.astype(np.uint8).reshape(k // 512, 16, n))


def unpack_weight(words, scales):
    g, p, n, _ = words.shape
    vals = np.ascontiguousarray(words).view(ml_dtypes.float8_e4m3fn).astype(np.float64) * np.repeat(np.exp2(scales.astype(np.float64) - 127.0), 8, axis=1)[..., None]
    return vals.transpose(0, 1, 3, 2).reshape(g * 512, n)


E2M1 = np.array([0.0, 0.5, 1.0, 1.5, 2.0, 3.0, 4.0, 6.0, -0.0, -0.5, -1.0, -1.5, -2.0, -3.0, -4.0, -6.0])


def pack_fp4(w):
    k, n = w.shape
    w = f64(np.asarray(w, np.float32).astype(ml_dtypes.bfloat16)).reshape(k // 32, 32, n)
    amax = np.abs(w).max(1)
    mant, ex = np.frexp(amax / 6.0)
    byte = np.clip(np.where(amax > 0, np.where(mant > 0.5, ex, ex - 1) + 127, 1), 1, 254)
    scaled = (w * np.exp2(127.0 - byte)[:, None, :]).reshape(k, n).astype(np.float32)
    c = np.ascontiguousarray(scaled.reshape(k // 512, 128, 4, n).transpose(0, 1, 3, 2)).astype(ml_dtypes.float4_e2m1fn).view(np.uint8) & 0xF
    words = (c[..., 0::2] | (c[..., 1::2] << 4)).reshape(k // 512, 128, 2 * n)
    return np.ascontiguousarray(words), np.ascontiguousarray(byte.astype(np.uint8).reshape(k // 512, 16, n))


def unpack_fp4(words, scales):
    g, _, n = scales.shape
    words = np.ascontiguousarray(words).reshape(g, 128, n, 2)
    nib = np.empty((g, 128, n, 4), np.uint8)
    nib[..., 0::2] = words & 0xF
    nib[..., 1::2] = words >> 4
    vals = E2M1[nib] * np.repeat(np.exp2(scales.astype(np.float64) - 127.0), 8, axis=1)[..., None]
    return vals.transpose(0, 1, 3, 2).reshape(g * 512, n)


def sigmoid(v):
    return 1.0 / (1.0 + np.exp(-np.maximum(v, -700.0)))

def planes(y):
    n, m = y.shape
    v = y.astype(np.float32).astype(ml_dtypes.bfloat16).astype(np.float64).reshape(n // 32, 32, m)
    top = np.abs(v).max(1)
    byte = np.clip(np.where(top > 0, np.frexp(top)[1] - 1 + 127 - 7, 1), 1, 254)
    codes = (v * np.exp2(127.0 - byte)[:, None, :]).reshape(n, m).astype(np.float32).astype(ml_dtypes.float8_e4m3fn).view(np.uint8)
    words = codes.reshape(n // 512, 128, 4, m).transpose(0, 1, 3, 2)
    return np.ascontiguousarray(words), np.ascontiguousarray(byte.astype(np.uint8).reshape(n // 512, 16, m))


K, T, S, H, C = 512, 2048, 512, 512, 512


def setup_inputs():
    n = np.random.standard_normal
    s = mx_kscale(K)[:, None]
    packed_xT = pack_weight(n((K, T)) * s)
    packed_w1 = pack_fp4(n((K, H)) / np.sqrt(K) / s)
    return {
        "x_words": packed_xT[0],
        "x_scales": packed_xT[1],
        "w1_words": packed_w1[0],
        "w1_scales": packed_w1[1],
        "sl": np.random.uniform(1.0, 2.0, (H, 1)).astype(np.float32),
        "th": (0.5 * n((H, 1))).astype(np.float32),
        "gs": (np.random.uniform(0.5, 1.5, (K, 1)) / s).astype(np.float32),
        "gs2": (np.random.uniform(0.5, 1.5, (K, 1)) / s).astype(np.float32),
        "offs": striped(np.random.permutation(T)[:S]),
        "n1": striped(np.random.permutation(S)),
        "n2": striped(np.random.permutation(S)),
        "n3": striped(np.random.permutation(S)),
        "ca": striped(np.random.permutation(T)[:C]),
        "cb": striped(np.random.permutation(T)[:C]),
        "n4": striped(np.random.permutation(S)),
        "n5": striped(np.random.permutation(S)),
        "n6": striped(np.random.permutation(S)),
    }


def reference(x_words, x_scales, w1_words, w1_scales, sl, th, gs, gs2, offs, n1, n2, n3, ca, cb, n4, n5, n6):
    x_cb = unpack_weight(x_words, x_scales)[:, unstriped(cb)]
    xq = unpack_weight(x_words, x_scales)[:, unstriped(offs)]
    y = unpack_fp4(w1_words, w1_scales).T @ xq
    sg = sigmoid(f64(sl) * (y[:, unstriped(n3)] - f64(th)))
    z2 = f64(gs2) * (y * sg)
    b = 0.0625 * ((x_cb.T @ mxq(z2, 0, "e4m3")))
    x_ca = unpack_weight(x_words, x_scales)[:, unstriped(ca)]
    z = f64(gs) * (0.75 * ((y - y[:, unstriped(n1)]) * (y - y[:, unstriped(n2)])))
    a = 0.0625 * ((x_ca.T @ mxq(z, 0, "e4m3")))
    out_0 = b * (a[:, unstriped(n4)] - a) + 0.5 * (b[:, unstriped(n6)] * (a[:, unstriped(n5)] - a))
    return (out_0,) + planes(out_0)

@@ -1,0 +1,283 @@
+from contextlib import ExitStack
+
+import concourse.mybir as mybir
+
+K, T, S, H, C = 512, 2048, 512, 512, 512
+FLOPS = 3 * 2 * 512 * 512 * 512
+
+F32 = mybir.dt.float32
+BF16 = mybir.dt.bfloat16
+I32 = mybir.dt.int32
+U32 = mybir.dt.uint32
+U16 = mybir.dt.uint16
+U8 = mybir.dt.uint8
+FP8X4 = mybir.dt.float8_e4m3fn_x4
+FP4X4 = mybir.dt.float4_e2m1fn_x4
+MULT = mybir.AluOpType.mult
+ADD = mybir.AluOpType.add
+SUB = mybir.AluOpType.subtract
+COPY = mybir.ActivationFunctionType.Copy
+SIGMOID = mybir.ActivationFunctionType.Sigmoid
+
+P = 128
+PACK = 4
+HALVES = 2
+W = S // HALVES
+LW = W // 16
+
+
+def tile_picked_twocdflowbquadesa_none_po_kernel(tc, x_words, x_scales, w1_words, w1_scales, sl, th, gs, gs2, offs, n1, n2, n3, ca, cb, n4, n5, n6, out_0, out_1, out_2):
+    nc = tc.nc
+    with ExitStack() as ctx:
+        sb = ctx.enter_context(tc.tile_pool(name="sb", bufs=1))
+        ps = ctx.enter_context(tc.psum_pool(name="ps", bufs=1))
+
+        def load_list(name, src):
+            tile = sb.tile([P, S // 16], U16, name=name)
+            nc.sync.dma_start(tile[:], src)
+            return tile
+
+        def load_scale_rows(tile, src):
+            for q in range(4):
+                nc.sync.dma_start(tile[32 * q : 32 * q + 4, :].bitcast(I32), src[0, 4 * q : 4 * q + 4, :].bitcast(I32))
+
+        def load_row_factor(name, src, queue):
+            tile = sb.tile([P, PACK], F32, name=name)
+            queue.dma_start(tile[:], src.rearrange("(p t) o -> p (t o)", t=PACK))
+            return tile
+
+        def half_list(lst, h):
+            return lst[:, h * LW : (h + 1) * LW]
+
+        def cols(h):
+            return slice(h * W, (h + 1) * W)
+
+        xs = sb.tile([P, T], U8, name="xs", align_bytes=64)
+        ws = sb.tile([P, H], U8, name="ws", align_bytes=64)
+        nc.vector.memset(xs[:].bitcast(I32), 0)
+        nc.vector.memset(ws[:].bitcast(I32), 0)
+        offs_l = load_list("offs_l", offs)
+        load_scale_rows(xs, x_scales)
+        ca_l = load_list("ca_l", ca)
+        ww = sb.tile([P, 2 * H], U8, name="ww", align_bytes=64)
+        nc.sync.dma_start(ww[:].bitcast(I32), w1_words[0].bitcast(I32))
+        xw = sb.tile([P, T], U32, name="xw", align_bytes=64)
+        nc.sync.dma_start(xw[:].bitcast(I32), x_words[0].rearrange("p n t -> p (n t)").bitcast(I32))
+        load_scale_rows(ws, w1_scales)
+        n3_l = load_list("n3_l", n3)
+        sl_t = load_row_factor("sl_t", sl, nc.gpsimd)
+        th_t = load_row_factor("th_t", th, nc.gpsimd)
+        n1_l = load_list("n1_l", n1)
+        n2_l = load_list("n2_l", n2)
+        gs_t = load_row_factor("gs_t", gs, nc.sync)
+        cb_l = load_list("cb_l", cb)
+        gs2_t = load_row_factor("gs2_t", gs2, nc.sync)
+        n4_l = load_list("n4_l", n4)
+        n5_l = load_list("n5_l", n5)
+        n6_l = load_list("n6_l", n6)
+
+        wwd = sb.tile([P, 2 * H], U8, name="wwd", align_bytes=64)
+        wsd = sb.tile([P, H], U8, name="wsd", align_bytes=64)
+        nc.gpsimd.tensor_copy(
+            out=wwd[:].rearrange("p (t m e) -> p t m e", t=PACK, e=2),
+            in_=ww[:].rearrange("p (m t e) -> p t m e", t=PACK, e=2),
+        )
+        nc.gpsimd.tensor_copy(
+            out=wsd[:].rearrange("p (t m) -> p t m", t=PACK),
+            in_=ws[:].rearrange("p (m t) -> p t m", t=PACK),
+        )
+        slth = sb.tile([P, PACK], F32, name="slth")
+        bias = sb.tile([P, PACK], F32, name="bias")
+        zfac = sb.tile([P, PACK], F32, name="zfac")
+        nc.gpsimd.tensor_tensor(slth[:], sl_t[:], th_t[:], MULT)
+        nc.gpsimd.tensor_scalar(bias[:], slth[:], -1.0, 0.0, MULT, ADD)
+        nc.gpsimd.tensor_scalar(zfac[:], gs_t[:], 0.75, 0.0, MULT, ADD)
+
+        def dealt(tile):
+            return tile[:].rearrange("p (t m) -> p m t", t=PACK)
+
+        xq_s = sb.tile([P, S], U8, name="xq_s", align_bytes=64)
+        ca_s = sb.tile([P, C], U8, name="ca_s", align_bytes=64)
+        cb_s = sb.tile([P, C], U8, name="cb_s", align_bytes=64)
+        ca_w = sb.tile([P, C], U32, name="ca_w", align_bytes=64)
+        cb_w = sb.tile([P, C], U32, name="cb_w", align_bytes=64)
+        xq_w = [sb.tile([P, W], U32, name=f"xq_w{h}", align_bytes=64) for h in range(HALVES)]
+        nc.vector.tensor_copy(xq_s[:], xs[:].indirect(offs_l[:]))
+        nc.vector.tensor_copy(dealt(ca_s), xs[:].indirect(ca_l[:]))
+        for h in range(HALVES):
+            nc.vector.tensor_copy(xq_w[h][:], xw[:].indirect(half_list(offs_l, h)))
+
+        y_ps = [ps.tile([P, S], F32, name=f"y_ps{t}", tag=f"yb{t}") for t in range(PACK)]
+        y = [sb.tile([P, S], F32, name=f"y{t}") for t in range(PACK)]
+        for t in range(PACK):
+            for h in range(HALVES):
+                nc.tensor.matmul_mx(
+                    out=y_ps[t][:, cols(h)],
+                    lhsT=wwd[:, 2 * P * t : 2 * P * (t + 1)].bitcast(FP4X4),
+                    lhsT_scale=wsd[:, P * t : P * (t + 1)],
+                    rhs=xq_w[h][:].bitcast(FP8X4),
+                    rhs_scale=xq_s[:, cols(h)],
+                    start=True,
+                    stop=True,
+                )
+
+        def f32_tile(name, t, h):
+            return sb.tile([P, W], F32, name=f"{name}_{t}_{h}")
+
+        steps = [(h, t) for h in range(HALVES) for t in range(PACK)]
+        sg = {}
+
+        def fetch_sg(h, t):
+            sg[h, t] = f32_tile("sg", t, h)
+            nc.scalar.activation(
+                sg[h, t][:], y[t][:].indirect(half_list(n3_l, h)), SIGMOID,
+                bias=bias[:, t : t + 1], scale=sl_t[:, t : t + 1],
+            )
+
+        def fetch(name, window, lst, h, t):
+            got = f32_tile(name, t, h)
+            nc.scalar.activation(got[:], window[:].indirect(half_list(lst, h)), COPY)
+            return got
+
+        def interleave(engine_copy, name, rows):
+            grouped = sb.tile([P, W * PACK], BF16, name=name, align_bytes=64)
+            engine_copy(
+                out=grouped[:].rearrange("p (c i t) -> p c t i", i=4, t=PACK),
+                in_=rows[:].rearrange("p t (c i) -> p c t i", i=4),
+            )
+            return grouped
+
+        def quantize(name, grouped):
+            codes = sb.tile([P, W], U32, name=name + "_w", align_bytes=64)
+            scales = sb.tile([P, W], U8, name=name + "_s", align_bytes=64)
+            nc.vector.quantize_mx(out=codes[:].bitcast(FP8X4), scales=scales[:], in_=grouped[:])
+            return codes, scales
+
+        def score(banks, words, scale_bytes, h, codes, scales):
+            for t in range(PACK):
+                nc.tensor.matmul_mx(
+                    out=banks[t][:, cols(h)],
+                    lhsT=words[:, P * t : P * (t + 1)].bitcast(FP8X4),
+                    lhsT_scale=scale_bytes[:, P * t : P * (t + 1)],
+                    rhs=codes[:].bitcast(FP8X4),
+                    rhs_scale=scales[:],
+                    start=True,
+                    stop=True,
+                )
+
+        nc.vector.tensor_copy(y[0][:], y_ps[0][:])
+        fetch_sg(0, 0)
+        nc.vector.tensor_copy(dealt(ca_w), xw[:].indirect(ca_l[:]))
+
+        a_ps = [ps.tile([P, S], F32, name=f"a_ps{t}", tag=f"ab{t}") for t in range(PACK)]
+        z_rows = [sb.tile([P, PACK, W], BF16, name=f"z_rows{h}") for h in range(HALVES)]
+        d = {}
+
+        def z_product(h, t):
+            d1, d2 = d[h, t]
+            nc.vector.scalar_tensor_tensor(z_rows[h][:, t, :], d1[:], zfac[:, t : t + 1], d2[:], MULT, MULT)
+
+        def z_close(h):
+            grouped = interleave(nc.vector.tensor_copy, f"z_g{h}", z_rows[h])
+            return grouped
+
+        z_grouped = {}
+        for i, (h, t) in enumerate(steps):
+            g1 = fetch("g1", y[t], n1_l, h, t)
+            g2 = fetch("g2", y[t], n2_l, h, t)
+            if h == 0 and t + 1 < PACK:
+                nc.scalar.activation(y[t + 1][:], y_ps[t + 1][:], COPY)
+            d1 = f32_tile("d1", t, h)
+            d2 = f32_tile("d2", t, h)
+            d[h, t] = (d1, d2)
+            nc.vector.tensor_tensor(d1[:], g1[:], y[t][:, cols(h)], SUB)
+            if i > 0:
+                z_product(*steps[i - 1])
+            nc.vector.tensor_tensor(d2[:], g2[:], y[t][:, cols(h)], SUB)
+            if (h, t) == (0, 1):
+                nc.vector.tensor_copy(dealt(cb_s), xs[:].indirect(cb_l[:]))
+            if (h, t) == (0, 2):
+                nc.vector.tensor_copy(dealt(cb_w), xw[:].indirect(cb_l[:]))
+            if (h, t) == (1, 0):
+                z_grouped[0] = z_close(0)
+            if (h, t) == (1, 1):
+                score(a_ps, ca_w, ca_s, 0, *quantize("z_q0", z_grouped[0]))
+        for h, t in steps[1:]:
+            fetch_sg(h, t)
+        z2_rows = [sb.tile([P, PACK, W], BF16, name=f"z2_rows{h}") for h in range(HALVES)]
+
+        def z2_product(h, t):
+            nc.vector.scalar_tensor_tensor(z2_rows[h][:, t, :], y[t][:, cols(h)], gs2_t[:, t : t + 1], sg[h, t][:], MULT, MULT)
+
+        z2_product(0, 0)
+        z_product(1, PACK - 1)
+        z2_product(0, 1)
+        z_grouped[1] = z_close(1)
+        z2_product(0, 2)
+        score(a_ps, ca_w, ca_s, 1, *quantize("z_q1", z_grouped[1]))
+        z2_product(0, 3)
+
+        b_ps = [ps.tile([P, S], F32, name=f"b_ps{t}", tag=f"yb{t}") for t in range(PACK)]
+        z2_product(1, 0)
+        z2_g0 = interleave(nc.vector.tensor_copy, "z2_g0", z2_rows[0])
+        z2_product(1, 1)
+        score(b_ps, cb_w, cb_s, 0, *quantize("z2_q0", z2_g0))
+        z2_product(1, 2)
+        z2_product(1, 3)
+
+        a = [sb.tile([P, S], F32, name=f"a{t}") for t in range(PACK)]
+        b = [sb.tile([P, S], F32, name=f"b{t}") for t in range(PACK)]
+        res = [sb.tile([P, PACK, W], F32, name=f"res{h}") for h in range(HALVES)]
+        out_rows = out_0.rearrange("(p t) j -> p t j", t=PACK)
+        out_words = out_1[0].rearrange("p n t -> p (n t)")
+        e, uv = {}, {}
+
+        def differences(h, t):
+            if h == 0:
+                nc.scalar.activation(a[t][:], a_ps[t][:], COPY, scale=0.0625)
+            g4 = fetch("g4", a[t], n4_l, h, t)
+            g5 = fetch("g5", a[t], n5_l, h, t)
+            e4 = f32_tile("e4", t, h)
+            e5 = f32_tile("e5", t, h)
+            e[h, t] = (e4, e5)
+            nc.vector.tensor_tensor(e4[:], g4[:], a[t][:, cols(h)], SUB)
+            nc.vector.tensor_tensor(e5[:], g5[:], a[t][:, cols(h)], SUB)
+
+        def products(h, t):
+            if h == 0:
+                nc.scalar.activation(b[t][:], b_ps[t][:], COPY, scale=0.0625)
+            e4, e5 = e[h, t]
+            u = f32_tile("u", t, h)
+            v = f32_tile("v", t, h)
+            uv[h, t] = (u, v)
+            nc.vector.tensor_tensor(u[:], b[t][:, cols(h)], e4[:], MULT)
+            nc.vector.tensor_tensor(v[:], b[t][:].indirect(half_list(n6_l, h)), e5[:], MULT)
+
+        def total(h, t):
+            u, v = uv[h, t]
+            nc.vector.scalar_tensor_tensor(res[h][:, t, :], v[:], 0.5, u[:], MULT, ADD)
+            nc.sync.dma_start(out_rows[:, t, cols(h)], res[h][:, t, :])
+
+        def hand_on(h, grouped):
+            codes, scales = quantize(f"res_q{h}", grouped)
+            nc.sync.dma_start(out_words[:, PACK * W * h : PACK * W * (h + 1)].bitcast(I32), codes[:].bitcast(I32))
+            for q in range(4):
+                queue = nc.sync if q % 2 else nc.scalar
+                queue.dma_start(out_2[0, 4 * q : 4 * q + 4, cols(h)].bitcast(I32), scales[32 * q : 32 * q + 4, :].bitcast(I32))
+
+        z2_g1 = interleave(nc.vector.tensor_copy, "z2_g1", z2_rows[1])
+        differences(0, 0)
+        score(b_ps, cb_w, cb_s, 1, *quantize("z2_q1", z2_g1))
+        res_g0 = None
+        for i, (h, t) in enumerate(steps):
+            if i + 1 < len(steps):
+                differences(*steps[i + 1])
+            if i > 0:
+                total(*steps[i - 1])
+            products(h, t)
+            if (h, t) == (1, 1):
+                res_g0 = interleave(nc.scalar.copy, "res_g0", res[0])
+            if (h, t) == (1, 3):
+                hand_on(0, res_g0)
+        total(*steps[-1])
+        hand_on(1, interleave(nc.vector.tensor_copy, "res_g1", res[1]))

@@ -24,6 +24,8 @@ PACK = 4
 HALVES = 2
 W = S // HALVES
 LW = W // 16
+Y_WINDOW = 2 * S
+AB_WINDOW = S + 16
 
 
 def tile_picked_twocdflowbquadesa_none_po_kernel(tc, x_words, x_scales, w1_words, w1_scales, sl, th, gs, gs2, offs, n1, n2, n3, ca, cb, n4, n5, n6, out_0, out_1, out_2):
@@ -37,13 +39,13 @@ def tile_picked_twocdflowbquadesa_none_po_kernel(tc, x_words, x_scales, w1_words
             nc.sync.dma_start(tile[:], src)
             return tile
 
-        def load_scale_rows(tile, src):
+        def load_scale_rows(tile, src, queue):
             for q in range(4):
-                nc.sync.dma_start(tile[32 * q : 32 * q + 4, :].bitcast(I32), src[0, 4 * q : 4 * q + 4, :].bitcast(I32))
+                queue.dma_start(tile[32 * q : 32 * q + 4, :].bitcast(I32), src[0, 4 * q : 4 * q + 4, :].bitcast(I32))
 
-        def load_row_factor(name, src, queue):
+        def load_row_factor(name, src):
             tile = sb.tile([P, PACK], F32, name=name)
-            queue.dma_start(tile[:], src.rearrange("(p t) o -> p (t o)", t=PACK))
+            nc.sync.dma_start(tile[:], src.rearrange("(p t) o -> p (t o)", t=PACK))
             return tile
 
         def half_list(lst, h):
@@ -54,27 +56,39 @@ def tile_picked_twocdflowbquadesa_none_po_kernel(tc, x_words, x_scales, w1_words
 
         xs = sb.tile([P, T], U8, name="xs", align_bytes=64)
         ws = sb.tile([P, H], U8, name="ws", align_bytes=64)
-        nc.vector.memset(xs[:].bitcast(I32), 0)
-        nc.vector.memset(ws[:].bitcast(I32), 0)
+        nc.gpsimd.memset(xs[:].bitcast(I32), 0)
+        nc.gpsimd.memset(ws[:].bitcast(I32), 0)
         offs_l = load_list("offs_l", offs)
-        load_scale_rows(xs, x_scales)
-        ca_l = load_list("ca_l", ca)
+        load_scale_rows(xs, x_scales, nc.sync)
         ww = sb.tile([P, 2 * H], U8, name="ww", align_bytes=64)
         nc.sync.dma_start(ww[:].bitcast(I32), w1_words[0].bitcast(I32))
+        ca_l = load_list("ca_l", ca)
         xw = sb.tile([P, T], U32, name="xw", align_bytes=64)
         nc.sync.dma_start(xw[:].bitcast(I32), x_words[0].rearrange("p n t -> p (n t)").bitcast(I32))
-        load_scale_rows(ws, w1_scales)
+        load_scale_rows(ws, w1_scales, nc.sync)
+        sl_t = load_row_factor("sl_t", sl)
+        th_t = load_row_factor("th_t", th)
         n3_l = load_list("n3_l", n3)
-        sl_t = load_row_factor("sl_t", sl, nc.gpsimd)
-        th_t = load_row_factor("th_t", th, nc.gpsimd)
         n1_l = load_list("n1_l", n1)
         n2_l = load_list("n2_l", n2)
-        gs_t = load_row_factor("gs_t", gs, nc.sync)
         cb_l = load_list("cb_l", cb)
-        gs2_t = load_row_factor("gs2_t", gs2, nc.sync)
+        gs2_t = load_row_factor("gs2_t", gs2)
+        gs_t = load_row_factor("gs_t", gs)
         n4_l = load_list("n4_l", n4)
         n5_l = load_list("n5_l", n5)
         n6_l = load_list("n6_l", n6)
+
+        def window(name, width, tag=None):
+            tile = sb.tile([P, width], F32, name=name, tag=tag or name, align_bytes=64)
+            nc.gpsimd.memset(tile[:, S:], 0.0)
+            return tile
+
+        a = [window(f"a{t}", AB_WINDOW) for t in range(2)]
+        b = [window(f"b{t}", AB_WINDOW) for t in range(PACK)]
+        y = [window(f"y{t}", Y_WINDOW) for t in range(PACK)]
+
+        warm = sb.tile([P, 1], F32, name="warm")
+        nc.scalar.activation(warm[:], a[0][:, S : S + 1], SIGMOID)
 
         wwd = sb.tile([P, 2 * H], U8, name="wwd", align_bytes=64)
         wsd = sb.tile([P, H], U8, name="wsd", align_bytes=64)
@@ -98,9 +112,6 @@ def tile_picked_twocdflowbquadesa_none_po_kernel(tc, x_words, x_scales, w1_words
 
         xq_s = sb.tile([P, S], U8, name="xq_s", align_bytes=64)
         ca_s = sb.tile([P, C], U8, name="ca_s", align_bytes=64)
-        cb_s = sb.tile([P, C], U8, name="cb_s", align_bytes=64)
-        ca_w = sb.tile([P, C], U32, name="ca_w", align_bytes=64)
-        cb_w = sb.tile([P, C], U32, name="cb_w", align_bytes=64)
         xq_w = [sb.tile([P, W], U32, name=f"xq_w{h}", align_bytes=64) for h in range(HALVES)]
         nc.vector.tensor_copy(xq_s[:], xs[:].indirect(offs_l[:]))
         nc.vector.tensor_copy(dealt(ca_s), xs[:].indirect(ca_l[:]))
@@ -108,7 +119,6 @@ def tile_picked_twocdflowbquadesa_none_po_kernel(tc, x_words, x_scales, w1_words
             nc.vector.tensor_copy(xq_w[h][:], xw[:].indirect(half_list(offs_l, h)))
 
         y_ps = [ps.tile([P, S], F32, name=f"y_ps{t}", tag=f"yb{t}") for t in range(PACK)]
-        y = [sb.tile([P, S], F32, name=f"y{t}") for t in range(PACK)]
         for t in range(PACK):
             for h in range(HALVES):
                 nc.tensor.matmul_mx(
@@ -121,29 +131,24 @@ def tile_picked_twocdflowbquadesa_none_po_kernel(tc, x_words, x_scales, w1_words
                     stop=True,
                 )
 
-        def f32_tile(name, t, h):
-            return sb.tile([P, W], F32, name=f"{name}_{t}_{h}")
+        def rows_tile(name, t, tag=None):
+            return sb.tile([P, S], F32, name=f"{name}_{t}", tag=tag or f"{name}_{t}", align_bytes=64)
 
-        steps = [(h, t) for h in range(HALVES) for t in range(PACK)]
-        sg = {}
-
-        def fetch_sg(h, t):
-            sg[h, t] = f32_tile("sg", t, h)
-            nc.scalar.activation(
-                sg[h, t][:], y[t][:].indirect(half_list(n3_l, h)), SIGMOID,
-                bias=bias[:, t : t + 1], scale=sl_t[:, t : t + 1],
-            )
-
-        def fetch(name, window, lst, h, t):
-            got = f32_tile(name, t, h)
-            nc.scalar.activation(got[:], window[:].indirect(half_list(lst, h)), COPY)
+        def fetch_sg(t):
+            got = rows_tile("sg", t)
+            nc.scalar.activation(got[:], y[t][:].indirect(n3_l[:]), SIGMOID, bias=bias[:, t : t + 1], scale=sl_t[:, t : t + 1])
             return got
 
-        def interleave(engine_copy, name, rows):
-            grouped = sb.tile([P, W * PACK], BF16, name=name, align_bytes=64)
+        def fetch(name, rows, lst, t, tag=None):
+            got = rows_tile(name, t, tag)
+            nc.scalar.activation(got[:], rows[:].indirect(lst[:]), COPY)
+            return got
+
+        def interleave(engine_copy, name, rows, h):
+            grouped = sb.tile([P, W * PACK], BF16, name=f"{name}_g{h}", align_bytes=64)
             engine_copy(
                 out=grouped[:].rearrange("p (c i t) -> p c t i", i=4, t=PACK),
-                in_=rows[:].rearrange("p t (c i) -> p c t i", i=4),
+                in_=rows[:, :, cols(h)].rearrange("p t (c i) -> p c t i", i=4),
             )
             return grouped
 
@@ -153,131 +158,157 @@ def tile_picked_twocdflowbquadesa_none_po_kernel(tc, x_words, x_scales, w1_words
             nc.vector.quantize_mx(out=codes[:].bitcast(FP8X4), scales=scales[:], in_=grouped[:])
             return codes, scales
 
-        def score(banks, words, scale_bytes, h, codes, scales):
+        def score(name, rows, banks, words, scale_bytes):
+            grouped = [interleave(nc.vector.tensor_copy, name, rows, h) for h in range(HALVES)]
+            planes = [quantize(f"{name}_q{h}", grouped[h]) for h in range(HALVES)]
             for t in range(PACK):
-                nc.tensor.matmul_mx(
-                    out=banks[t][:, cols(h)],
-                    lhsT=words[:, P * t : P * (t + 1)].bitcast(FP8X4),
-                    lhsT_scale=scale_bytes[:, P * t : P * (t + 1)],
-                    rhs=codes[:].bitcast(FP8X4),
-                    rhs_scale=scales[:],
-                    start=True,
-                    stop=True,
-                )
+                for h in range(HALVES):
+                    nc.tensor.matmul_mx(
+                        out=banks[t][:, cols(h)],
+                        lhsT=words[:, P * t : P * (t + 1)].bitcast(FP8X4),
+                        lhsT_scale=scale_bytes[:, P * t : P * (t + 1)],
+                        rhs=planes[h][0][:].bitcast(FP8X4),
+                        rhs_scale=planes[h][1][:],
+                        start=True,
+                        stop=True,
+                    )
 
-        nc.vector.tensor_copy(y[0][:], y_ps[0][:])
-        fetch_sg(0, 0)
+        LAST = PACK - 1
+        nc.scalar.activation(y[0][:, :S], y_ps[0][:], COPY)
+        for t in range(1, PACK):
+            nc.vector.tensor_copy(y[t][:, :S], y_ps[t][:])
+        sg = {0: fetch_sg(0)}
+        g1, g2 = {}, {}
+        for t in range(PACK):
+            g1[t] = fetch("g1", y[t], n1_l, t)
+            g2[t] = fetch("g2", y[t], n2_l, t)
+        for t in range(1, PACK):
+            sg[t] = fetch_sg(t)
+
+        z_rows = sb.tile([P, PACK, S], BF16, name="z_rows")
+        d1 = [rows_tile("d1", t) for t in range(PACK)]
+        d2 = [rows_tile("d2", t) for t in range(PACK)]
+        every = slice(0, S)
+
+        def less(out, got, window, span=every):
+            nc.vector.tensor_tensor(out[:, span], got[:, span], window[:, span], SUB)
+
+        def z_product(t, span=every):
+            nc.vector.scalar_tensor_tensor(z_rows[:, t, span], d1[t][:, span], zfac[:, t : t + 1], d2[t][:, span], MULT, MULT)
+
+        def z2_product(t, span=every):
+            nc.vector.scalar_tensor_tensor(z2_rows[:, t, span], y[t][:, span], gs2_t[:, t : t + 1], sg[t][:, span], MULT, MULT)
+
+        cb_s = sb.tile([P, C], U8, name="cb_s", align_bytes=64)
+        ca_w = sb.tile([P, C], U32, name="ca_w", align_bytes=64)
+        cb_w = sb.tile([P, C], U32, name="cb_w", align_bytes=64)
         nc.vector.tensor_copy(dealt(ca_w), xw[:].indirect(ca_l[:]))
-
+        less(d1[0], g1[0], y[0])
+        nc.vector.tensor_copy(dealt(cb_s), xs[:].indirect(cb_l[:]))
+        less(d2[0], g2[0], y[0])
+        z_product(0)
+        less(d1[1], g1[1], y[1])
+        nc.vector.tensor_copy(dealt(cb_w), xw[:].indirect(cb_l[:]))
+        less(d2[1], g2[1], y[1])
+        less(d1[2], g1[2], y[2])
+        z_product(1)
+        less(d2[2], g2[2], y[2])
+        less(d1[3], g1[3], y[3])
+        z_product(2)
+        for h in range(HALVES):
+            less(d2[LAST], g2[LAST], y[LAST], cols(h))
+        for h in range(HALVES):
+            z_product(LAST, cols(h))
         a_ps = [ps.tile([P, S], F32, name=f"a_ps{t}", tag=f"ab{t}") for t in range(PACK)]
-        z_rows = [sb.tile([P, PACK, W], BF16, name=f"z_rows{h}") for h in range(HALVES)]
-        d = {}
-
-        def z_product(h, t):
-            d1, d2 = d[h, t]
-            nc.vector.scalar_tensor_tensor(z_rows[h][:, t, :], d1[:], zfac[:, t : t + 1], d2[:], MULT, MULT)
-
-        def z_close(h):
-            grouped = interleave(nc.vector.tensor_copy, f"z_g{h}", z_rows[h])
-            return grouped
-
-        z_grouped = {}
-        for i, (h, t) in enumerate(steps):
-            g1 = fetch("g1", y[t], n1_l, h, t)
-            g2 = fetch("g2", y[t], n2_l, h, t)
-            if h == 0 and t + 1 < PACK:
-                nc.scalar.activation(y[t + 1][:], y_ps[t + 1][:], COPY)
-            d1 = f32_tile("d1", t, h)
-            d2 = f32_tile("d2", t, h)
-            d[h, t] = (d1, d2)
-            nc.vector.tensor_tensor(d1[:], g1[:], y[t][:, cols(h)], SUB)
-            if i > 0:
-                z_product(*steps[i - 1])
-            nc.vector.tensor_tensor(d2[:], g2[:], y[t][:, cols(h)], SUB)
-            if (h, t) == (0, 1):
-                nc.vector.tensor_copy(dealt(cb_s), xs[:].indirect(cb_l[:]))
-            if (h, t) == (0, 2):
-                nc.vector.tensor_copy(dealt(cb_w), xw[:].indirect(cb_l[:]))
-            if (h, t) == (1, 0):
-                z_grouped[0] = z_close(0)
-            if (h, t) == (1, 1):
-                score(a_ps, ca_w, ca_s, 0, *quantize("z_q0", z_grouped[0]))
-        for h, t in steps[1:]:
-            fetch_sg(h, t)
-        z2_rows = [sb.tile([P, PACK, W], BF16, name=f"z2_rows{h}") for h in range(HALVES)]
-
-        def z2_product(h, t):
-            nc.vector.scalar_tensor_tensor(z2_rows[h][:, t, :], y[t][:, cols(h)], gs2_t[:, t : t + 1], sg[h, t][:], MULT, MULT)
-
-        z2_product(0, 0)
-        z_product(1, PACK - 1)
-        z2_product(0, 1)
-        z_grouped[1] = z_close(1)
-        z2_product(0, 2)
-        score(a_ps, ca_w, ca_s, 1, *quantize("z_q1", z_grouped[1]))
-        z2_product(0, 3)
-
+        score("z", z_rows, a_ps, ca_w, ca_s)
+        z2_rows = sb.tile([P, PACK, S], BF16, name="z2_rows", tag="z_g0", align_bytes=64)
+        for t in range(LAST):
+            z2_product(t)
+        for h in range(HALVES):
+            z2_product(LAST, cols(h))
         b_ps = [ps.tile([P, S], F32, name=f"b_ps{t}", tag=f"yb{t}") for t in range(PACK)]
-        z2_product(1, 0)
-        z2_g0 = interleave(nc.vector.tensor_copy, "z2_g0", z2_rows[0])
-        z2_product(1, 1)
-        score(b_ps, cb_w, cb_s, 0, *quantize("z2_q0", z2_g0))
-        z2_product(1, 2)
-        z2_product(1, 3)
+        score("z2", z2_rows, b_ps, cb_w, cb_s)
 
-        a = [sb.tile([P, S], F32, name=f"a{t}") for t in range(PACK)]
-        b = [sb.tile([P, S], F32, name=f"b{t}") for t in range(PACK)]
-        res = [sb.tile([P, PACK, W], F32, name=f"res{h}") for h in range(HALVES)]
+        res = sb.tile([P, PACK, S], F32, name="res")
         out_rows = out_0.rearrange("(p t) j -> p t j", t=PACK)
         out_words = out_1[0].rearrange("p n t -> p (n t)")
-        e, uv = {}, {}
+        g4, g5 = {}, {}
+        a.append(window("a2", AB_WINDOW, "z2_q1_w"))
+        a.append(window("a3", AB_WINDOW, "z2_q1_s"))
 
-        def differences(h, t):
-            if h == 0:
-                nc.scalar.activation(a[t][:], a_ps[t][:], COPY, scale=0.0625)
-            g4 = fetch("g4", a[t], n4_l, h, t)
-            g5 = fetch("g5", a[t], n5_l, h, t)
-            e4 = f32_tile("e4", t, h)
-            e5 = f32_tile("e5", t, h)
-            e[h, t] = (e4, e5)
-            nc.vector.tensor_tensor(e4[:], g4[:], a[t][:, cols(h)], SUB)
-            nc.vector.tensor_tensor(e5[:], g5[:], a[t][:, cols(h)], SUB)
+        def a_out(t):
+            nc.scalar.activation(a[t][:, :S], a_ps[t][:], COPY, scale=0.0625)
 
-        def products(h, t):
-            if h == 0:
-                nc.scalar.activation(b[t][:], b_ps[t][:], COPY, scale=0.0625)
-            e4, e5 = e[h, t]
-            u = f32_tile("u", t, h)
-            v = f32_tile("v", t, h)
-            uv[h, t] = (u, v)
-            nc.vector.tensor_tensor(u[:], b[t][:, cols(h)], e4[:], MULT)
-            nc.vector.tensor_tensor(v[:], b[t][:].indirect(half_list(n6_l, h)), e5[:], MULT)
+        def b_out(t):
+            nc.scalar.activation(b[t][:, :S], b_ps[t][:], COPY, scale=0.03125)
 
-        def total(h, t):
-            u, v = uv[h, t]
-            nc.vector.scalar_tensor_tensor(res[h][:, t, :], v[:], 0.5, u[:], MULT, ADD)
-            nc.sync.dma_start(out_rows[:, t, cols(h)], res[h][:, t, :])
+        a_out(0)
+        g4[0] = fetch("g4", a[0], n4_l, 0)
+        g5[0] = fetch("g5", a[0], n5_l, 0)
+        a_out(1)
+        g4[1] = fetch("g4", a[1], n4_l, 1)
+        b_out(0)
+        b_out(1)
+        g5[1] = fetch("g5", a[1], n5_l, 1, "cb_s")
+        a_out(2)
+        b_out(2)
+        g4[2] = fetch("g4", a[2], n4_l, 2)
+        g5[2] = fetch("g5", a[2], n5_l, 2)
+        a_out(LAST)
+        b_out(LAST)
+        g4[LAST] = fetch("g4", a[LAST], n4_l, LAST)
+        g5[LAST] = rows_tile("g5", LAST)
+        for h in range(HALVES):
+            nc.scalar.activation(g5[LAST][:, cols(h)], a[LAST][:].indirect(half_list(n5_l, h)), COPY)
 
-        def hand_on(h, grouped):
-            codes, scales = quantize(f"res_q{h}", grouped)
-            nc.sync.dma_start(out_words[:, PACK * W * h : PACK * W * (h + 1)].bitcast(I32), codes[:].bitcast(I32))
-            for q in range(4):
-                queue = nc.sync if q % 2 else nc.scalar
-                queue.dma_start(out_2[0, 4 * q : 4 * q + 4, cols(h)].bitcast(I32), scales[32 * q : 32 * q + 4, :].bitcast(I32))
+        e4 = [rows_tile("e4", t, "z2_g1" if t == 1 else None) for t in range(PACK)]
+        e5 = [rows_tile("e5", t, "z2_g0" if t == 0 else None) for t in range(PACK)]
+        u = [rows_tile("u", t) for t in range(PACK)]
+        v = [rows_tile("v", t) for t in range(PACK)]
 
-        z2_g1 = interleave(nc.vector.tensor_copy, "z2_g1", z2_rows[1])
-        differences(0, 0)
-        score(b_ps, cb_w, cb_s, 1, *quantize("z2_q1", z2_g1))
-        res_g0 = None
-        for i, (h, t) in enumerate(steps):
-            if i + 1 < len(steps):
-                differences(*steps[i + 1])
-            if i > 0:
-                total(*steps[i - 1])
-            products(h, t)
-            if (h, t) == (1, 1):
-                res_g0 = interleave(nc.scalar.copy, "res_g0", res[0])
-            if (h, t) == (1, 3):
-                hand_on(0, res_g0)
-        total(*steps[-1])
-        hand_on(1, interleave(nc.vector.tensor_copy, "res_g1", res[1]))
+        def a_less(out, got, t, span=every):
+            nc.vector.scalar_tensor_tensor(out[:, span], a_ps[t][:, span], 0.0625, got[:, span], MULT, SUB)
+
+        def own_term(t):
+            nc.vector.scalar_tensor_tensor(u[t][:], b_ps[t][:], -0.0625, e4[t][:], MULT, MULT)
+
+        def total(engine, t, span=every):
+            engine.tensor_tensor(res[:, t, span], u[t][:, span], v[t][:, span], SUB)
+            nc.sync.dma_start(out_rows[:, t, span], res[:, t, span])
+
+        def other_term(t):
+            nc.vector.tensor_tensor(v[t][:], b[t][:].indirect(n6_l[:]), e5[t][:], MULT)
+
+        a_less(e4[0], g4[0], 0)
+        a_less(e5[0], g5[0], 0)
+        a_less(e4[1], g4[1], 1)
+        own_term(0)
+        other_term(0)
+        total(nc.gpsimd, 0)
+        own_term(1)
+        a_less(e5[1], g5[1], 1)
+        other_term(1)
+        total(nc.gpsimd, 1)
+        a_less(e4[2], g4[2], 2)
+        own_term(2)
+        a_less(e5[2], g5[2], 2)
+        other_term(2)
+        total(nc.gpsimd, 2)
+        a_less(e4[LAST], g4[LAST], LAST)
+        a_less(e5[LAST], g5[LAST], LAST, cols(0))
+        own_term(LAST)
+        a_less(e5[LAST], g5[LAST], LAST, cols(1))
+        for h in range(HALVES):
+            nc.vector.tensor_tensor(v[LAST][:, cols(h)], b[LAST][:].indirect(half_list(n6_l, h)), e5[LAST][:, cols(h)], MULT)
+        for h in range(HALVES):
+            total(nc.vector, LAST, cols(h))
+        first = interleave(nc.scalar.copy, "res", res, 0)
+        second = interleave(nc.vector.tensor_copy, "res", res, 1)
+        res_w = sb.tile([P, S], U32, name="res_w", align_bytes=64)
+        res_s = sb.tile([P, S], U8, name="res_s", align_bytes=64)
+        for h, grouped in ((1, second), (0, first)):
+            nc.vector.quantize_mx(out=res_w[:, cols(h)].bitcast(FP8X4), scales=res_s[:, cols(h)], in_=grouped[:])
+            nc.sync.dma_start(out_words[:, PACK * W * h : PACK * W * (h + 1)].bitcast(I32), res_w[:, cols(h)].bitcast(I32))
+        for q in range(4):
+            queue = nc.sync if q % 2 else nc.scalar
+            queue.dma_start(out_2[0, 4 * q : 4 * q + 4, :].bitcast(I32), res_s[32 * q : 32 * q + 4, :].bitcast(I32))

from contextlib import ExitStack

import concourse.mybir as mybir

K, T, S, H, C = 512, 2048, 512, 512, 512
FLOPS = 3 * 2 * 512 * 512 * 512

F32 = mybir.dt.float32
BF16 = mybir.dt.bfloat16
I32 = mybir.dt.int32
U32 = mybir.dt.uint32
U16 = mybir.dt.uint16
U8 = mybir.dt.uint8
FP8X4 = mybir.dt.float8_e4m3fn_x4
FP4X4 = mybir.dt.float4_e2m1fn_x4
MULT = mybir.AluOpType.mult
ADD = mybir.AluOpType.add
SUB = mybir.AluOpType.subtract
COPY = mybir.ActivationFunctionType.Copy
SIGMOID = mybir.ActivationFunctionType.Sigmoid

P = 128
PACK = 4
HALVES = 2
W = S // HALVES
LW = W // 16
Y_WINDOW = 2 * S
AB_WINDOW = S + 16


def tile_picked_twocdflowbquadesa_none_po_kernel(tc, x_words, x_scales, w1_words, w1_scales, sl, th, gs, gs2, offs, n1, n2, n3, ca, cb, n4, n5, n6, out_0, out_1, out_2):
    nc = tc.nc
    with ExitStack() as ctx:
        sb = ctx.enter_context(tc.tile_pool(name="sb", bufs=1))
        ps = ctx.enter_context(tc.psum_pool(name="ps", bufs=1))

        def load_list(name, src):
            tile = sb.tile([P, S // 16], U16, name=name)
            nc.sync.dma_start(tile[:], src)
            return tile

        def load_scale_rows(tile, src, queue):
            for q in range(4):
                queue.dma_start(tile[32 * q : 32 * q + 4, :].bitcast(I32), src[0, 4 * q : 4 * q + 4, :].bitcast(I32))

        def load_row_factor(name, src):
            tile = sb.tile([P, PACK], F32, name=name)
            nc.sync.dma_start(tile[:], src.rearrange("(p t) o -> p (t o)", t=PACK))
            return tile

        def half_list(lst, h):
            return lst[:, h * LW : (h + 1) * LW]

        def cols(h):
            return slice(h * W, (h + 1) * W)

        xs = sb.tile([P, T], U8, name="xs", align_bytes=64)
        ws = sb.tile([P, H], U8, name="ws", align_bytes=64)
        nc.gpsimd.memset(xs[:].bitcast(I32), 0)
        nc.gpsimd.memset(ws[:].bitcast(I32), 0)
        offs_l = load_list("offs_l", offs)
        load_scale_rows(xs, x_scales, nc.sync)
        ww = sb.tile([P, 2 * H], U8, name="ww", align_bytes=64)
        nc.sync.dma_start(ww[:].bitcast(I32), w1_words[0].bitcast(I32))
        ca_l = load_list("ca_l", ca)
        xw = sb.tile([P, T], U32, name="xw", align_bytes=64)
        nc.sync.dma_start(xw[:].bitcast(I32), x_words[0].rearrange("p n t -> p (n t)").bitcast(I32))
        load_scale_rows(ws, w1_scales, nc.sync)
        sl_t = load_row_factor("sl_t", sl)
        th_t = load_row_factor("th_t", th)
        n3_l = load_list("n3_l", n3)
        n1_l = load_list("n1_l", n1)
        n2_l = load_list("n2_l", n2)
        cb_l = load_list("cb_l", cb)
        gs2_t = load_row_factor("gs2_t", gs2)
        gs_t = load_row_factor("gs_t", gs)
        n4_l = load_list("n4_l", n4)
        n5_l = load_list("n5_l", n5)
        n6_l = load_list("n6_l", n6)

        def window(name, width, tag=None):
            tile = sb.tile([P, width], F32, name=name, tag=tag or name, align_bytes=64)
            nc.gpsimd.memset(tile[:, S:], 0.0)
            return tile

        a = [window(f"a{t}", AB_WINDOW) for t in range(2)]
        b = [window(f"b{t}", AB_WINDOW) for t in range(PACK)]
        y = [window(f"y{t}", Y_WINDOW) for t in range(PACK)]

        warm = sb.tile([P, 1], F32, name="warm")
        nc.scalar.activation(warm[:], a[0][:, S : S + 1], SIGMOID)

        wwd = sb.tile([P, 2 * H], U8, name="wwd", align_bytes=64)
        wsd = sb.tile([P, H], U8, name="wsd", align_bytes=64)
        nc.gpsimd.tensor_copy(
            out=wwd[:].rearrange("p (t m e) -> p t m e", t=PACK, e=2),
            in_=ww[:].rearrange("p (m t e) -> p t m e", t=PACK, e=2),
        )
        nc.gpsimd.tensor_copy(
            out=wsd[:].rearrange("p (t m) -> p t m", t=PACK),
            in_=ws[:].rearrange("p (m t) -> p t m", t=PACK),
        )
        slth = sb.tile([P, PACK], F32, name="slth")
        bias = sb.tile([P, PACK], F32, name="bias")
        zfac = sb.tile([P, PACK], F32, name="zfac")
        nc.gpsimd.tensor_tensor(slth[:], sl_t[:], th_t[:], MULT)
        nc.gpsimd.tensor_scalar(bias[:], slth[:], -1.0, 0.0, MULT, ADD)
        nc.gpsimd.tensor_scalar(zfac[:], gs_t[:], 0.75, 0.0, MULT, ADD)

        def dealt(tile):
            return tile[:].rearrange("p (t m) -> p m t", t=PACK)

        xq_s = sb.tile([P, S], U8, name="xq_s", align_bytes=64)
        ca_s = sb.tile([P, C], U8, name="ca_s", align_bytes=64)
        xq_w = [sb.tile([P, W], U32, name=f"xq_w{h}", align_bytes=64) for h in range(HALVES)]
        nc.vector.tensor_copy(xq_s[:], xs[:].indirect(offs_l[:]))
        nc.vector.tensor_copy(dealt(ca_s), xs[:].indirect(ca_l[:]))
        for h in range(HALVES):
            nc.vector.tensor_copy(xq_w[h][:], xw[:].indirect(half_list(offs_l, h)))

        y_ps = [ps.tile([P, S], F32, name=f"y_ps{t}", tag=f"yb{t}") for t in range(PACK)]
        for t in range(PACK):
            for h in range(HALVES):
                nc.tensor.matmul_mx(
                    out=y_ps[t][:, cols(h)],
                    lhsT=wwd[:, 2 * P * t : 2 * P * (t + 1)].bitcast(FP4X4),
                    lhsT_scale=wsd[:, P * t : P * (t + 1)],
                    rhs=xq_w[h][:].bitcast(FP8X4),
                    rhs_scale=xq_s[:, cols(h)],
                    start=True,
                    stop=True,
                )

        def rows_tile(name, t, tag=None):
            return sb.tile([P, S], F32, name=f"{name}_{t}", tag=tag or f"{name}_{t}", align_bytes=64)

        def fetch_sg(t):
            got = rows_tile("sg", t)
            nc.scalar.activation(got[:], y[t][:].indirect(n3_l[:]), SIGMOID, bias=bias[:, t : t + 1], scale=sl_t[:, t : t + 1])
            return got

        def fetch(name, rows, lst, t, tag=None):
            got = rows_tile(name, t, tag)
            nc.scalar.activation(got[:], rows[:].indirect(lst[:]), COPY)
            return got

        def interleave(engine_copy, name, rows, h):
            grouped = sb.tile([P, W * PACK], BF16, name=f"{name}_g{h}", align_bytes=64)
            engine_copy(
                out=grouped[:].rearrange("p (c i t) -> p c t i", i=4, t=PACK),
                in_=rows[:, :, cols(h)].rearrange("p t (c i) -> p c t i", i=4),
            )
            return grouped

        def quantize(name, grouped):
            codes = sb.tile([P, W], U32, name=name + "_w", align_bytes=64)
            scales = sb.tile([P, W], U8, name=name + "_s", align_bytes=64)
            nc.vector.quantize_mx(out=codes[:].bitcast(FP8X4), scales=scales[:], in_=grouped[:])
            return codes, scales

        def score(name, rows, banks, words, scale_bytes):
            grouped = [interleave(nc.vector.tensor_copy, name, rows, h) for h in range(HALVES)]
            planes = [quantize(f"{name}_q{h}", grouped[h]) for h in range(HALVES)]
            for t in range(PACK):
                for h in range(HALVES):
                    nc.tensor.matmul_mx(
                        out=banks[t][:, cols(h)],
                        lhsT=words[:, P * t : P * (t + 1)].bitcast(FP8X4),
                        lhsT_scale=scale_bytes[:, P * t : P * (t + 1)],
                        rhs=planes[h][0][:].bitcast(FP8X4),
                        rhs_scale=planes[h][1][:],
                        start=True,
                        stop=True,
                    )

        LAST = PACK - 1
        nc.scalar.activation(y[0][:, :S], y_ps[0][:], COPY)
        for t in range(1, PACK):
            nc.vector.tensor_copy(y[t][:, :S], y_ps[t][:])
        sg = {0: fetch_sg(0)}
        g1, g2 = {}, {}
        for t in range(PACK):
            g1[t] = fetch("g1", y[t], n1_l, t)
            g2[t] = fetch("g2", y[t], n2_l, t)
        for t in range(1, PACK):
            sg[t] = fetch_sg(t)

        z_rows = sb.tile([P, PACK, S], BF16, name="z_rows")
        d1 = [rows_tile("d1", t) for t in range(PACK)]
        d2 = [rows_tile("d2", t) for t in range(PACK)]
        every = slice(0, S)

        def less(out, got, window, span=every):
            nc.vector.tensor_tensor(out[:, span], got[:, span], window[:, span], SUB)

        def z_product(t, span=every):
            nc.vector.scalar_tensor_tensor(z_rows[:, t, span], d1[t][:, span], zfac[:, t : t + 1], d2[t][:, span], MULT, MULT)

        def z2_product(t, span=every):
            nc.vector.scalar_tensor_tensor(z2_rows[:, t, span], y[t][:, span], gs2_t[:, t : t + 1], sg[t][:, span], MULT, MULT)

        cb_s = sb.tile([P, C], U8, name="cb_s", align_bytes=64)
        ca_w = sb.tile([P, C], U32, name="ca_w", align_bytes=64)
        cb_w = sb.tile([P, C], U32, name="cb_w", align_bytes=64)
        nc.vector.tensor_copy(dealt(ca_w), xw[:].indirect(ca_l[:]))
        less(d1[0], g1[0], y[0])
        nc.vector.tensor_copy(dealt(cb_s), xs[:].indirect(cb_l[:]))
        less(d2[0], g2[0], y[0])
        z_product(0)
        less(d1[1], g1[1], y[1])
        nc.vector.tensor_copy(dealt(cb_w), xw[:].indirect(cb_l[:]))
        less(d2[1], g2[1], y[1])
        less(d1[2], g1[2], y[2])
        z_product(1)
        less(d2[2], g2[2], y[2])
        less(d1[3], g1[3], y[3])
        z_product(2)
        for h in range(HALVES):
            less(d2[LAST], g2[LAST], y[LAST], cols(h))
        for h in range(HALVES):
            z_product(LAST, cols(h))
        a_ps = [ps.tile([P, S], F32, name=f"a_ps{t}", tag=f"ab{t}") for t in range(PACK)]
        score("z", z_rows, a_ps, ca_w, ca_s)
        z2_rows = sb.tile([P, PACK, S], BF16, name="z2_rows", tag="z_g0", align_bytes=64)
        for t in range(LAST):
            z2_product(t)
        for h in range(HALVES):
            z2_product(LAST, cols(h))
        b_ps = [ps.tile([P, S], F32, name=f"b_ps{t}", tag=f"yb{t}") for t in range(PACK)]
        score("z2", z2_rows, b_ps, cb_w, cb_s)

        res = sb.tile([P, PACK, S], F32, name="res")
        out_rows = out_0.rearrange("(p t) j -> p t j", t=PACK)
        out_words = out_1[0].rearrange("p n t -> p (n t)")
        g4, g5 = {}, {}
        a.append(window("a2", AB_WINDOW, "z2_q1_w"))
        a.append(window("a3", AB_WINDOW, "z2_q1_s"))

        def a_out(t):
            nc.scalar.activation(a[t][:, :S], a_ps[t][:], COPY, scale=0.0625)

        def b_out(t):
            nc.scalar.activation(b[t][:, :S], b_ps[t][:], COPY, scale=0.03125)

        a_out(0)
        g4[0] = fetch("g4", a[0], n4_l, 0)
        g5[0] = fetch("g5", a[0], n5_l, 0)
        a_out(1)
        g4[1] = fetch("g4", a[1], n4_l, 1)
        b_out(0)
        b_out(1)
        g5[1] = fetch("g5", a[1], n5_l, 1, "cb_s")
        a_out(2)
        b_out(2)
        g4[2] = fetch("g4", a[2], n4_l, 2)
        g5[2] = fetch("g5", a[2], n5_l, 2)
        a_out(LAST)
        b_out(LAST)
        g4[LAST] = fetch("g4", a[LAST], n4_l, LAST)
        g5[LAST] = rows_tile("g5", LAST)
        for h in range(HALVES):
            nc.scalar.activation(g5[LAST][:, cols(h)], a[LAST][:].indirect(half_list(n5_l, h)), COPY)

        e4 = [rows_tile("e4", t, "z2_g1" if t == 1 else None) for t in range(PACK)]
        e5 = [rows_tile("e5", t, "z2_g0" if t == 0 else None) for t in range(PACK)]
        u = [rows_tile("u", t) for t in range(PACK)]
        v = [rows_tile("v", t) for t in range(PACK)]

        def a_less(out, got, t, span=every):
            nc.vector.scalar_tensor_tensor(out[:, span], a_ps[t][:, span], 0.0625, got[:, span], MULT, SUB)

        def own_term(t):
            nc.vector.scalar_tensor_tensor(u[t][:], b_ps[t][:], -0.0625, e4[t][:], MULT, MULT)

        def total(engine, t, span=every):
            engine.tensor_tensor(res[:, t, span], u[t][:, span], v[t][:, span], SUB)
            nc.sync.dma_start(out_rows[:, t, span], res[:, t, span])

        def other_term(t):
            nc.vector.tensor_tensor(v[t][:], b[t][:].indirect(n6_l[:]), e5[t][:], MULT)

        a_less(e4[0], g4[0], 0)
        a_less(e5[0], g5[0], 0)
        a_less(e4[1], g4[1], 1)
        own_term(0)
        other_term(0)
        total(nc.gpsimd, 0)
        own_term(1)
        a_less(e5[1], g5[1], 1)
        other_term(1)
        total(nc.gpsimd, 1)
        a_less(e4[2], g4[2], 2)
        own_term(2)
        a_less(e5[2], g5[2], 2)
        other_term(2)
        total(nc.gpsimd, 2)
        a_less(e4[LAST], g4[LAST], LAST)
        a_less(e5[LAST], g5[LAST], LAST, cols(0))
        own_term(LAST)
        a_less(e5[LAST], g5[LAST], LAST, cols(1))
        for h in range(HALVES):
            nc.vector.tensor_tensor(v[LAST][:, cols(h)], b[LAST][:].indirect(half_list(n6_l, h)), e5[LAST][:, cols(h)], MULT)
        for h in range(HALVES):
            total(nc.vector, LAST, cols(h))
        first = interleave(nc.scalar.copy, "res", res, 0)
        second = interleave(nc.vector.tensor_copy, "res", res, 1)
        res_w = sb.tile([P, S], U32, name="res_w", align_bytes=64)
        res_s = sb.tile([P, S], U8, name="res_s", align_bytes=64)
        for h, grouped in ((1, second), (0, first)):
            nc.vector.quantize_mx(out=res_w[:, cols(h)].bitcast(FP8X4), scales=res_s[:, cols(h)], in_=grouped[:])
            nc.sync.dma_start(out_words[:, PACK * W * h : PACK * W * (h + 1)].bitcast(I32), res_w[:, cols(h)].bitcast(I32))
        for q in range(4):
            queue = nc.sync if q % 2 else nc.scalar
            queue.dma_start(out_2[0, 4 * q : 4 * q + 4, :].bitcast(I32), res_s[32 * q : 32 * q + 4, :].bitcast(I32))
